import numpy as np
import ml_dtypes


def mxq(x, axis, fmt="e4m3"):
    dtype, down = {"e4m3": (ml_dtypes.float8_e4m3fn, 7), "e5m2": (ml_dtypes.float8_e5m2, 14)}[fmt]
    v = np.moveaxis(np.asarray(x, np.float32).astype(ml_dtypes.bfloat16).astype(np.float64), axis, -1)
    blocks = v.reshape(v.shape[:-1] + (-1, 32))
    amax = np.abs(blocks).max(-1, keepdims=True)
    byte = np.maximum(np.where(amax > 0, np.frexp(amax)[1] - 1 + 127, 0) - down, 1)
    scale = np.exp2(byte - 127.0)
    codes = (blocks / scale).astype(np.float32).astype(dtype).astype(np.float64)
    return np.moveaxis((codes * scale).reshape(v.shape), -1, axis)


WIDE = False


def mx_kscale(k):
    if not WIDE:
        return np.ones(k)
    levels = np.array([10, -10, 5, -5, 0])
    if k % 512:
        return np.exp2(np.random.permutation(np.resize(levels, k // 32))).repeat(32)
    a = np.empty((k // 512, 16))
    for p in range(k // 512):
        a[p, :8] = np.random.permutation(np.resize(levels, 8))
        for g in range(8):
            far = levels[np.abs(levels - a[p, g]) >= 10]
            a[p, g + 8] = far[np.random.randint(len(far))]
    return np.exp2(a.ravel()).repeat(32)


def f64(x):
    return np.asarray(x).astype(np.float64)


def striped(idx):
    return np.tile(idx.reshape(-1, 16).T, (8, 1)).astype(np.uint16)


def unstriped(offs):
    return offs[:16].T.reshape(-1).astype(np.int64)


def pack_weight(w):
    k, n = w.shape
    w = f64(np.asarray(w, np.float32).astype(ml_dtypes.bfloat16)).reshape(k // 32, 32, n)
    amax = np.abs(w).max(1)
    byte = np.clip(np.where(amax > 0, np.frexp(amax)[1] - 1 + 127 - 7, 1), 1, 254)
    scaled = (w * np.exp2(127.0 - byte)[:, None, :]).reshape(k, n).astype(np.float32)
    words = np.ascontiguousarray(scaled.reshape(k // 512, 128, 4, n).transpose(0, 1, 3, 2)).astype(ml_dtypes.float8_e4m3fn).view(np.uint8)
    return words, np.ascontiguousarray(byte.astype(np.uint8).reshape(k // 512, 16, n))


def unpack_weight(words, scales):
    g, p, n, _ = words.shape
    vals = np.ascontiguousarray(words).view(ml_dtypes.float8_e4m3fn).astype(np.float64) * np.repeat(np.exp2(scales.astype(np.float64) - 127.0), 8, axis=1)[..., None]
    return vals.transpose(0, 1, 3, 2).reshape(g * 512, n)


def relu(v):
    return np.maximum(v, 0.0)


def sigmoid(v):
    return 1.0 / (1.0 + np.exp(-np.maximum(v, -700.0)))


K, T, S, H, N = 512, 2048, 512, 512, 128


def setup_inputs():
    n = np.random.standard_normal
    s = mx_kscale(K)[:, None]
    u = mx_kscale(H)
    packed_xT = pack_weight(n((K, T)) * s)
    return {
        "x_words": packed_xT[0],
        "x_scales": packed_xT[1],
        "w1": (n((K, H)) / np.sqrt(K) / s * u).astype(np.float32),
        "w2": (n((K, H)) / np.sqrt(K) / s).astype(np.float32),
        "w3": (n((H, N)) / np.sqrt(H) / u[:, None]).astype(np.float32),
        "offs": striped(np.random.permutation(T)[:S]),
        "dst": striped(np.random.permutation(T)[:S]),
    }


def reference(x_words, x_scales, w1, w2, w3, offs, dst):
    xq = unpack_weight(x_words, x_scales)[:, unstriped(offs)]
    y = relu(mxq(f64(w1), 0, "e4m3").T @ xq)
    x_dst = unpack_weight(x_words, x_scales)[:, unstriped(dst)]
    e = np.tanh(mxq(f64(w2), 0, "e4m3").T @ x_dst)
    z = y * e
    return sigmoid(mxq(f64(w3), 0, "e4m3").T @ mxq(z, 0, "e4m3"))

@@ -1,0 +1,153 @@
+from contextlib import ExitStack
+
+import concourse.mybir as mybir
+
+K, T, S, H, N = 512, 2048, 512, 512, 128
+FLOPS = 2 * K * H * S * 2 + 2 * H * N * S
+
+F32 = mybir.dt.float32
+BF16 = mybir.dt.bfloat16
+I32 = mybir.dt.int32
+U32 = mybir.dt.uint32
+U16 = mybir.dt.uint16
+U8 = mybir.dt.uint8
+FP8X4 = mybir.dt.float8_e4m3fn_x4
+ACT = mybir.ActivationFunctionType
+ALU = mybir.AluOpType
+
+P = 128
+PACK = 4
+CHUNK = 128
+HALF = 256
+
+
+def tile_picked_zlmlp_tanh_p_kernel(tc, x_words, x_scales, w1, w2, w3, offs, dst, out):
+    nc = tc.nc
+    with ExitStack() as ctx:
+        lists = ctx.enter_context(tc.tile_pool(name="lists", bufs=1))
+        sb = ctx.enter_context(tc.tile_pool(name="sb", bufs=1))
+        psum = ctx.enter_context(tc.psum_pool(name="psum", bufs=1))
+
+        dst_list = lists.tile([P, S // 16], U16, name="dst_list")
+        nc.sync.dma_start(dst_list[:], dst)
+        src_list = lists.tile([P, S // 16], U16, name="src_list")
+        nc.sync.dma_start(src_list[:], offs)
+
+        scale_table = sb.tile([P, T], U8, name="scale_table", align_bytes=64)
+        nc.vector.memset(scale_table[:].bitcast(I32), 0)
+        word_table = sb.tile([P, T], I32, name="word_table", align_bytes=64)
+        words_hbm = x_words[0].rearrange("p n t -> p (n t)").bitcast(I32)
+        nc.sync.dma_start(word_table[:, :T // 2], words_hbm[:, :T // 2])
+        for r in range(4):
+            nc.sync.dma_start(scale_table[r:P:32, :].bitcast(I32), x_scales[0, r:16:4, :].bitcast(I32))
+        nc.sync.dma_start(word_table[:, T // 2:], words_hbm[:, T // 2:])
+
+        warm_in = sb.tile([P, 8], F32, name="warm_in")
+        nc.vector.memset(warm_in[:], 0.0)
+        warm_out = sb.tile([P, 8], F32, name="warm_out")
+        nc.scalar.activation(warm_out[:], warm_in[:], ACT.Sigmoid)
+
+        w2_raw = sb.tile([P, PACK, H], F32, name="w2_raw", tag="raw_b")
+        nc.sync.dma_start(w2_raw[:], w2.rearrange("(p j) c -> p j c", j=PACK))
+        w1_raw = sb.tile([P, PACK, H], F32, name="w1_raw", tag="raw_a")
+        nc.sync.dma_start(w1_raw[:], w1.rearrange("(p j) c -> p j c", j=PACK))
+
+        def gather_scales(lst, name):
+            got = sb.tile([P, S], U8, name=name, align_bytes=64)
+            nc.vector.tensor_copy(got[:], scale_table[:].indirect(lst[:]))
+            return got
+
+        def gather_words(lst, h, name):
+            got = sb.tile([P, HALF], U32, name=name, align_bytes=64)
+            cols = HALF // 16
+            nc.vector.tensor_copy(got[:], word_table[:].bitcast(U32).indirect(lst[:, h * cols:(h + 1) * cols]))
+            return got
+
+        def round_slots(rounded, raw, t0, t1, on_vector):
+            src = raw[:].rearrange("p j (u t r) -> p t u j r", t=PACK, r=4)[:, t0:t1]
+            lo = t0 % 2
+            to = rounded[:].rearrange("p (t u r j) -> p t u j r", t=2, r=4, j=PACK)[:, lo:lo + t1 - t0]
+            if on_vector:
+                nc.vector.tensor_copy(to, src)
+            else:
+                nc.scalar.copy(to, src)
+
+        def quantise(rounded, width, name):
+            codes = sb.tile([P, width], U32, name=name + "_codes", align_bytes=64)
+            scales = sb.tile([P, width], U8, name=name + "_scales", align_bytes=64)
+            nc.vector.quantize_mx(out=codes[:].bitcast(FP8X4), scales=scales[:], in_=rounded[:])
+            return codes, scales
+
+        def product(bank_cols, stat, lo, words, scales):
+            nc.tensor.matmul_mx(out=bank_cols, lhsT=stat[0][:, lo:lo + P].bitcast(FP8X4), lhsT_scale=stat[1][:, lo:lo + P],
+                                rhs=words.bitcast(FP8X4), rhs_scale=scales, start=True, stop=True)
+
+        dst_scales = gather_scales(dst_list, "dst_scales")
+        src_scales = gather_scales(src_list, "src_scales")
+        dst_words = [gather_words(dst_list, h, "dst_words%d" % h) for h in range(2)]
+        src_words = [gather_words(src_list, 0, "src_words0")]
+
+        w2_bf = [sb.tile([P, 2 * PACK * P], BF16, name="w2_bf%d" % a, align_bytes=64) for a in range(2)]
+        round_slots(w2_bf[0], w2_raw, 0, 2, False)
+        round_slots(w2_bf[1], w2_raw, 2, 3, False)
+        round_slots(w2_bf[1], w2_raw, 3, 4, True)
+        w2_q = [quantise(w2_bf[a], 2 * P, "w2_q%d" % a) for a in range(2)]
+
+        w3_raw = sb.tile([P, PACK, N], F32, name="w3_raw", tag="raw_b")
+        w3_rows = w3.rearrange("(u t r) n -> r u t n", t=PACK, r=4)
+        for r in range(4):
+            nc.sync.dma_start(w3_raw[r:P:4, :, :], w3_rows[r])
+
+
+        n_chunks = S // CHUNK
+        e_bank = [psum.tile([P, PACK, CHUNK], F32, name="e_bank%d" % c) for c in range(n_chunks)]
+        y_bank = [psum.tile([P, PACK, CHUNK], F32, name="y_bank%d" % c) for c in range(n_chunks)]
+
+        def first_layer(bank, c, w_q, words, scales):
+            lo = (c % 2) * CHUNK
+            for t in range(PACK):
+                product(bank[c][:, t, :], w_q[t // 2], (t % 2) * P, words[c // 2][:, lo:lo + CHUNK], scales[:, c * CHUNK:(c + 1) * CHUNK])
+
+        def tanh_chunk(c):
+            nc.scalar.activation(e_vals[:, c], e_bank[c][:].rearrange("p t n -> p n t"), ACT.Tanh)
+
+        for c in range(n_chunks):
+            first_layer(e_bank, c, w2_q, dst_words, dst_scales)
+
+        w1_bf = [sb.tile([P, 2 * PACK * P], BF16, name="w1_bf%d" % a, align_bytes=64) for a in range(2)]
+        round_slots(w1_bf[0], w1_raw, 0, 2, True)
+        round_slots(w1_bf[1], w1_raw, 2, 4, False)
+        w1_q = [quantise(w1_bf[a], 2 * P, "w1_q%d" % a) for a in range(2)]
+        src_words.append(gather_words(src_list, 1, "w1_bf1"))
+        e_vals = sb.tile([P, n_chunks, CHUNK, PACK], F32, name="e_vals", tag="raw_a")
+        for c in range(n_chunks):
+            tanh_chunk(c)
+        for c in range(n_chunks):
+            first_layer(y_bank, c, w1_q, src_words, src_scales)
+
+        w3_bf = sb.tile([P, N * PACK], BF16, name="w3_bf", align_bytes=64)
+        nc.scalar.copy(w3_bf[:].rearrange("p (c i t) -> p c t i", i=4, t=PACK),
+                       w3_raw[:].rearrange("p t (c i) -> p c t i", i=4))
+
+        z_bf = []
+
+        def gate(c):
+            z = sb.tile([P, CHUNK * PACK], BF16, name="z_bf%d" % c, align_bytes=64)
+            nc.vector.scalar_tensor_tensor(z[:].rearrange("p (n t) -> p n t", t=PACK),
+                                           y_bank[c][:].rearrange("p t n -> p n t"), 0.0, e_vals[:, c],
+                                           ALU.max, ALU.mult)
+            z_bf.append(z)
+
+        def finish(c, w3_q):
+            z_q = quantise(z_bf[c], CHUNK, "z_q%d" % c)
+            product(e_bank[c][:, 0, :], w3_q, 0, z_q[0][:], z_q[1][:])
+            res = sb.tile([P, CHUNK], F32, name="res%d" % c)
+            nc.scalar.activation(res[:], e_bank[c][:, 0, :], ACT.Sigmoid)
+            nc.sync.dma_start(out[:, c * CHUNK:(c + 1) * CHUNK], res[:])
+
+        gate(0)
+        w3_q = quantise(w3_bf, N, "w3_q")
+        for c in range(1, n_chunks):
+            gate(c)
+            finish(c - 1, w3_q)
+        finish(n_chunks - 1, w3_q)

@@ -28,19 +28,19 @@ def tile_picked_zlmlp_tanh_p_kernel(tc, x_words, x_scales, w1, w2, w3, offs, dst
         sb = ctx.enter_context(tc.tile_pool(name="sb", bufs=1))
         psum = ctx.enter_context(tc.psum_pool(name="psum", bufs=1))
 
-        dst_list = lists.tile([P, S // 16], U16, name="dst_list")
-        nc.sync.dma_start(dst_list[:], dst)
-        src_list = lists.tile([P, S // 16], U16, name="src_list")
-        nc.sync.dma_start(src_list[:], offs)
 
         scale_table = sb.tile([P, T], U8, name="scale_table", align_bytes=64)
         nc.vector.memset(scale_table[:].bitcast(I32), 0)
         word_table = sb.tile([P, T], I32, name="word_table", align_bytes=64)
         words_hbm = x_words[0].rearrange("p n t -> p (n t)").bitcast(I32)
-        nc.sync.dma_start(word_table[:, :T // 2], words_hbm[:, :T // 2])
+        nc.sync.dma_start(word_table[:, :T // 4], words_hbm[:, :T // 4])
+        dst_list = lists.tile([P, S // 16], U16, name="dst_list")
+        nc.sync.dma_start(dst_list[:], dst)
+        src_list = lists.tile([P, S // 16], U16, name="src_list")
+        nc.sync.dma_start(src_list[:], offs)
         for r in range(4):
             nc.sync.dma_start(scale_table[r:P:32, :].bitcast(I32), x_scales[0, r:16:4, :].bitcast(I32))
-        nc.sync.dma_start(word_table[:, T // 2:], words_hbm[:, T // 2:])
+        nc.sync.dma_start(word_table[:, T // 4:], words_hbm[:, T // 4:])
 
         warm_in = sb.tile([P, 8], F32, name="warm_in")
         nc.vector.memset(warm_in[:], 0.0)
@@ -58,7 +58,7 @@ def tile_picked_zlmlp_tanh_p_kernel(tc, x_words, x_scales, w1, w2, w3, offs, dst
             return got
 
         def gather_words(lst, h, name):
-            got = sb.tile([P, HALF], U32, name=name, align_bytes=64)
+            got = sb.tile([P, HALF], U32, name=name, tag=name, align_bytes=64)
             cols = HALF // 16
             nc.vector.tensor_copy(got[:], word_table[:].bitcast(U32).indirect(lst[:, h * cols:(h + 1) * cols]))
             return got
@@ -88,22 +88,23 @@ def tile_picked_zlmlp_tanh_p_kernel(tc, x_words, x_scales, w1, w2, w3, offs, dst
         src_words = [gather_words(src_list, 0, "src_words0")]
 
         w2_bf = [sb.tile([P, 2 * PACK * P], BF16, name="w2_bf%d" % a, align_bytes=64) for a in range(2)]
-        round_slots(w2_bf[0], w2_raw, 0, 2, False)
-        round_slots(w2_bf[1], w2_raw, 2, 3, False)
-        round_slots(w2_bf[1], w2_raw, 3, 4, True)
+        round_slots(w2_bf[0], w2_raw, 0, 2, True)
+        round_slots(w2_bf[1], w2_raw, 2, 4, False)
         w2_q = [quantise(w2_bf[a], 2 * P, "w2_q%d" % a) for a in range(2)]
 
-        w3_raw = sb.tile([P, PACK, N], F32, name="w3_raw", tag="raw_b")
+        w3_raw = sb.tile([P, PACK, N], F32, name="w3_raw")
         w3_rows = w3.rearrange("(u t r) n -> r u t n", t=PACK, r=4)
         for r in range(4):
             nc.sync.dma_start(w3_raw[r:P:4, :, :], w3_rows[r])
 
 
         n_chunks = S // CHUNK
-        e_bank = [psum.tile([P, PACK, CHUNK], F32, name="e_bank%d" % c) for c in range(n_chunks)]
-        y_bank = [psum.tile([P, PACK, CHUNK], F32, name="y_bank%d" % c) for c in range(n_chunks)]
+        e_bank = []
+        y_bank = []
 
-        def first_layer(bank, c, w_q, words, scales):
+        def first_layer(bank, slot, w_q, words, scales):
+            c = len(bank)
+            bank.append(psum.tile([P, PACK, CHUNK], F32, name="first_layer", tag="bank%d" % slot))
             lo = (c % 2) * CHUNK
             for t in range(PACK):
                 product(bank[c][:, t, :], w_q[t // 2], (t % 2) * P, words[c // 2][:, lo:lo + CHUNK], scales[:, c * CHUNK:(c + 1) * CHUNK])
@@ -111,23 +112,27 @@ def tile_picked_zlmlp_tanh_p_kernel(tc, x_words, x_scales, w1, w2, w3, offs, dst
         def tanh_chunk(c):
             nc.scalar.activation(e_vals[:, c], e_bank[c][:].rearrange("p t n -> p n t"), ACT.Tanh)
 
-        for c in range(n_chunks):
+        for c in range(n_chunks - 1):
             first_layer(e_bank, c, w2_q, dst_words, dst_scales)
 
-        w1_bf = [sb.tile([P, 2 * PACK * P], BF16, name="w1_bf%d" % a, align_bytes=64) for a in range(2)]
+        w1_bf = [sb.tile([P, 2 * PACK * P], BF16, name="w1_bf%d" % a, tag="w1_bf%d" % a, align_bytes=64) for a in range(2)]
         round_slots(w1_bf[0], w1_raw, 0, 2, True)
         round_slots(w1_bf[1], w1_raw, 2, 4, False)
         w1_q = [quantise(w1_bf[a], 2 * P, "w1_q%d" % a) for a in range(2)]
         src_words.append(gather_words(src_list, 1, "w1_bf1"))
         e_vals = sb.tile([P, n_chunks, CHUNK, PACK], F32, name="e_vals", tag="raw_a")
-        for c in range(n_chunks):
-            tanh_chunk(c)
-        for c in range(n_chunks):
-            first_layer(y_bank, c, w1_q, src_words, src_scales)
-
-        w3_bf = sb.tile([P, N * PACK], BF16, name="w3_bf", align_bytes=64)
+        first_layer(y_bank, 3, w1_q, src_words, src_scales)
+        first_layer(y_bank, 4, w1_q, src_words, src_scales)
+        tanh_chunk(0)
+        first_layer(e_bank, 0, w2_q, dst_words, dst_scales)
+        tanh_chunk(1)
+        first_layer(y_bank, 1, w1_q, src_words, src_scales)
+        w3_bf = sb.tile([P, N * PACK], BF16, name="w3_bf", tag="dst_words1", align_bytes=64)
         nc.scalar.copy(w3_bf[:].rearrange("p (c i t) -> p c t i", i=4, t=PACK),
                        w3_raw[:].rearrange("p t (c i) -> p c t i", i=4))
+        tanh_chunk(2)
+        first_layer(y_bank, 2, w1_q, src_words, src_scales)
+        tanh_chunk(3)
 
         z_bf = []
 
@@ -140,9 +145,10 @@ def tile_picked_zlmlp_tanh_p_kernel(tc, x_words, x_scales, w1, w2, w3, offs, dst
 
         def finish(c, w3_q):
             z_q = quantise(z_bf[c], CHUNK, "z_q%d" % c)
-            product(e_bank[c][:, 0, :], w3_q, 0, z_q[0][:], z_q[1][:])
+            o_bank = psum.tile([P, CHUNK], F32, name="o_bank", bufs=3)
+            product(o_bank[:], w3_q, 0, z_q[0][:], z_q[1][:])
             res = sb.tile([P, CHUNK], F32, name="res%d" % c)
-            nc.scalar.activation(res[:], e_bank[c][:, 0, :], ACT.Sigmoid)
+            nc.scalar.activation(res[:], o_bank[:], ACT.Sigmoid)
             nc.sync.dma_start(out[:, c * CHUNK:(c + 1) * CHUNK], res[:])
 
         gate(0)

@@ -49,8 +49,11 @@ def tile_picked_zlmlp_tanh_p_kernel(tc, x_words, x_scales, w1, w2, w3, offs, dst
 
         w2_raw = sb.tile([P, PACK, H], F32, name="w2_raw", tag="raw_b")
         nc.sync.dma_start(w2_raw[:], w2.rearrange("(p j) c -> p j c", j=PACK))
-        w1_raw = sb.tile([P, PACK, H], F32, name="w1_raw", tag="raw_a")
-        nc.sync.dma_start(w1_raw[:], w1.rearrange("(p j) c -> p j c", j=PACK))
+        w1_rows = w1.rearrange("(p j) c -> p j c", j=PACK)
+        w1_raw = []
+        for g in range(2):
+            w1_raw.append(sb.tile([P, 2, H], F32, name="w1_raw%d" % g, tag="w1_raw%d" % g))
+            nc.sync.dma_start(w1_raw[g][:], w1_rows[:, 2 * g:2 * g + 2, :])
 
         def gather_scales(lst, name):
             got = sb.tile([P, S], U8, name=name, align_bytes=64)
@@ -63,10 +66,9 @@ def tile_picked_zlmlp_tanh_p_kernel(tc, x_words, x_scales, w1, w2, w3, offs, dst
             nc.vector.tensor_copy(got[:], word_table[:].bitcast(U32).indirect(lst[:, h * cols:(h + 1) * cols]))
             return got
 
-        def round_slots(rounded, raw, t0, t1, on_vector):
+        def round_slots(rounded, raw, t0, t1, on_vector, j0=0, j1=PACK):
             src = raw[:].rearrange("p j (u t r) -> p t u j r", t=PACK, r=4)[:, t0:t1]
-            lo = t0 % 2
-            to = rounded[:].rearrange("p (t u r j) -> p t u j r", t=2, r=4, j=PACK)[:, lo:lo + t1 - t0]
+            to = rounded[:].rearrange("p (t u r j) -> p t u j r", t=2, r=4, j=PACK)[:, :, :, j0:j1, :]
             if on_vector:
                 nc.vector.tensor_copy(to, src)
             else:
@@ -92,7 +94,7 @@ def tile_picked_zlmlp_tanh_p_kernel(tc, x_words, x_scales, w1, w2, w3, offs, dst
         round_slots(w2_bf[1], w2_raw, 2, 4, False)
         w2_q = [quantise(w2_bf[a], 2 * P, "w2_q%d" % a) for a in range(2)]
 
-        w3_raw = sb.tile([P, PACK, N], F32, name="w3_raw")
+        w3_raw = sb.tile([P, PACK, N], F32, name="w3_raw", tag="w3_raw")
         w3_rows = w3.rearrange("(u t r) n -> r u t n", t=PACK, r=4)
         for r in range(4):
             nc.sync.dma_start(w3_raw[r:P:4, :, :], w3_rows[r])
@@ -110,28 +112,30 @@ def tile_picked_zlmlp_tanh_p_kernel(tc, x_words, x_scales, w1, w2, w3, offs, dst
                 product(bank[c][:, t, :], w_q[t // 2], (t % 2) * P, words[c // 2][:, lo:lo + CHUNK], scales[:, c * CHUNK:(c + 1) * CHUNK])
 
         def tanh_chunk(c):
-            nc.scalar.activation(e_vals[:, c], e_bank[c][:].rearrange("p t n -> p n t"), ACT.Tanh)
+            nc.scalar.activation(e_vals[c // 2][:, c % 2], e_bank[c][:].rearrange("p t n -> p n t"), ACT.Tanh)
 
         for c in range(n_chunks - 1):
             first_layer(e_bank, c, w2_q, dst_words, dst_scales)
 
         w1_bf = [sb.tile([P, 2 * PACK * P], BF16, name="w1_bf%d" % a, tag="w1_bf%d" % a, align_bytes=64) for a in range(2)]
-        round_slots(w1_bf[0], w1_raw, 0, 2, True)
-        round_slots(w1_bf[1], w1_raw, 2, 4, False)
+        for g in range(2):
+            round_slots(w1_bf[0], w1_raw[g], 0, 2, True, 2 * g, 2 * g + 2)
+            round_slots(w1_bf[1], w1_raw[g], 2, 4, False, 2 * g, 2 * g + 2)
         w1_q = [quantise(w1_bf[a], 2 * P, "w1_q%d" % a) for a in range(2)]
         src_words.append(gather_words(src_list, 1, "w1_bf1"))
-        e_vals = sb.tile([P, n_chunks, CHUNK, PACK], F32, name="e_vals", tag="raw_a")
+        e_vals = [sb.tile([P, 2, CHUNK, PACK], F32, name="e_vals0", tag="w1_raw1")]
         first_layer(y_bank, 3, w1_q, src_words, src_scales)
         first_layer(y_bank, 4, w1_q, src_words, src_scales)
         tanh_chunk(0)
         first_layer(e_bank, 0, w2_q, dst_words, dst_scales)
         tanh_chunk(1)
-        first_layer(y_bank, 1, w1_q, src_words, src_scales)
-        w3_bf = sb.tile([P, N * PACK], BF16, name="w3_bf", tag="dst_words1", align_bytes=64)
+        first_layer(y_bank, 5, w1_q, src_words, src_scales)
+        w3_bf = sb.tile([P, N * PACK], BF16, name="w3_bf", align_bytes=64)
         nc.scalar.copy(w3_bf[:].rearrange("p (c i t) -> p c t i", i=4, t=PACK),
                        w3_raw[:].rearrange("p t (c i) -> p c t i", i=4))
+        e_vals.append(sb.tile([P, 2, CHUNK, PACK], F32, name="e_vals1", tag="w3_raw"))
         tanh_chunk(2)
-        first_layer(y_bank, 2, w1_q, src_words, src_scales)
+        first_layer(y_bank, 6, w1_q, src_words, src_scales)
         tanh_chunk(3)
 
         z_bf = []
@@ -139,13 +143,13 @@ def tile_picked_zlmlp_tanh_p_kernel(tc, x_words, x_scales, w1, w2, w3, offs, dst
         def gate(c):
             z = sb.tile([P, CHUNK * PACK], BF16, name="z_bf%d" % c, align_bytes=64)
             nc.vector.scalar_tensor_tensor(z[:].rearrange("p (n t) -> p n t", t=PACK),
-                                           y_bank[c][:].rearrange("p t n -> p n t"), 0.0, e_vals[:, c],
+                                           y_bank[c][:].rearrange("p t n -> p n t"), 0.0, e_vals[c // 2][:, c % 2],
                                            ALU.max, ALU.mult)
             z_bf.append(z)
 
         def finish(c, w3_q):
             z_q = quantise(z_bf[c], CHUNK, "z_q%d" % c)
-            o_bank = psum.tile([P, CHUNK], F32, name="o_bank", bufs=3)
+            o_bank = psum.tile([P, CHUNK], F32, name="o_bank", tag="bank%d" % (3 + c))
             product(o_bank[:], w3_q, 0, z_q[0][:], z_q[1][:])
             res = sb.tile([P, CHUNK], F32, name="res%d" % c)
             nc.scalar.activation(res[:], o_bank[:], ACT.Sigmoid)

@@ -31,7 +31,7 @@ def tile_picked_zlmlp_tanh_p_kernel(tc, x_words, x_scales, w1, w2, w3, offs, dst
 
         scale_table = sb.tile([P, T], U8, name="scale_table", align_bytes=64)
         nc.vector.memset(scale_table[:].bitcast(I32), 0)
-        word_table = sb.tile([P, T], I32, name="word_table", align_bytes=64)
+        word_table = sb.tile([P, T], I32, name="word_table", tag="word_table", align_bytes=64)
         words_hbm = x_words[0].rearrange("p n t -> p (n t)").bitcast(I32)
         nc.sync.dma_start(word_table[:, :T // 4], words_hbm[:, :T // 4])
         dst_list = lists.tile([P, S // 16], U16, name="dst_list")
@@ -94,7 +94,7 @@ def tile_picked_zlmlp_tanh_p_kernel(tc, x_words, x_scales, w1, w2, w3, offs, dst
         round_slots(w2_bf[1], w2_raw, 2, 4, False)
         w2_q = [quantise(w2_bf[a], 2 * P, "w2_q%d" % a) for a in range(2)]
 
-        w3_raw = sb.tile([P, PACK, N], F32, name="w3_raw", tag="w3_raw")
+        w3_raw = sb.tile([P, PACK, N], F32, name="w3_raw")
         w3_rows = w3.rearrange("(u t r) n -> r u t n", t=PACK, r=4)
         for r in range(4):
             nc.sync.dma_start(w3_raw[r:P:4, :, :], w3_rows[r])
@@ -112,7 +112,7 @@ def tile_picked_zlmlp_tanh_p_kernel(tc, x_words, x_scales, w1, w2, w3, offs, dst
                 product(bank[c][:, t, :], w_q[t // 2], (t % 2) * P, words[c // 2][:, lo:lo + CHUNK], scales[:, c * CHUNK:(c + 1) * CHUNK])
 
         def tanh_chunk(c):
-            nc.scalar.activation(e_vals[c // 2][:, c % 2], e_bank[c][:].rearrange("p t n -> p n t"), ACT.Tanh)
+            nc.scalar.activation(e_vals[:, c], e_bank[c][:].rearrange("p t n -> p n t"), ACT.Tanh)
 
         for c in range(n_chunks - 1):
             first_layer(e_bank, c, w2_q, dst_words, dst_scales)
@@ -123,17 +123,16 @@ def tile_picked_zlmlp_tanh_p_kernel(tc, x_words, x_scales, w1, w2, w3, offs, dst
             round_slots(w1_bf[1], w1_raw[g], 2, 4, False, 2 * g, 2 * g + 2)
         w1_q = [quantise(w1_bf[a], 2 * P, "w1_q%d" % a) for a in range(2)]
         src_words.append(gather_words(src_list, 1, "w1_bf1"))
-        e_vals = [sb.tile([P, 2, CHUNK, PACK], F32, name="e_vals0", tag="w1_raw1")]
+        e_vals = sb.tile([P, n_chunks, CHUNK, PACK], F32, name="e_vals", tag="w1_raw1")
         first_layer(y_bank, 3, w1_q, src_words, src_scales)
         first_layer(y_bank, 4, w1_q, src_words, src_scales)
         tanh_chunk(0)
         first_layer(e_bank, 0, w2_q, dst_words, dst_scales)
         tanh_chunk(1)
         first_layer(y_bank, 5, w1_q, src_words, src_scales)
-        w3_bf = sb.tile([P, N * PACK], BF16, name="w3_bf", align_bytes=64)
-        nc.scalar.copy(w3_bf[:].rearrange("p (c i t) -> p c t i", i=4, t=PACK),
-                       w3_raw[:].rearrange("p t (c i) -> p c t i", i=4))
-        e_vals.append(sb.tile([P, 2, CHUNK, PACK], F32, name="e_vals1", tag="w3_raw"))
+        w3_bf = sb.tile([P, N * PACK], BF16, name="w3_bf", tag="word_table", align_bytes=64)
+        nc.gpsimd.tensor_scalar(w3_bf[:].rearrange("p (n t) -> p n t", t=PACK),
+                                w3_raw[:].rearrange("p t n -> p n t"), 1.0, 0.0, ALU.mult, ALU.add)
         tanh_chunk(2)
         first_layer(y_bank, 6, w1_q, src_words, src_scales)
         tanh_chunk(3)
@@ -143,7 +142,7 @@ def tile_picked_zlmlp_tanh_p_kernel(tc, x_words, x_scales, w1, w2, w3, offs, dst
         def gate(c):
             z = sb.tile([P, CHUNK * PACK], BF16, name="z_bf%d" % c, align_bytes=64)
             nc.vector.scalar_tensor_tensor(z[:].rearrange("p (n t) -> p n t", t=PACK),
-                                           y_bank[c][:].rearrange("p t n -> p n t"), 0.0, e_vals[c // 2][:, c % 2],
+                                           y_bank[c][:].rearrange("p t n -> p n t"), 0.0, e_vals[:, c],
                                            ALU.max, ALU.mult)
             z_bf.append(z)
 

from contextlib import ExitStack

import concourse.mybir as mybir

K, T, S, H, N = 512, 2048, 512, 512, 128
FLOPS = 2 * K * H * S * 2 + 2 * H * N * S

F32 = mybir.dt.float32
BF16 = mybir.dt.bfloat16
I32 = mybir.dt.int32
U32 = mybir.dt.uint32
U16 = mybir.dt.uint16
U8 = mybir.dt.uint8
FP8X4 = mybir.dt.float8_e4m3fn_x4
ACT = mybir.ActivationFunctionType
ALU = mybir.AluOpType

P = 128
PACK = 4
CHUNK = 128
HALF = 256


def tile_picked_zlmlp_tanh_p_kernel(tc, x_words, x_scales, w1, w2, w3, offs, dst, out):
    nc = tc.nc
    with ExitStack() as ctx:
        lists = ctx.enter_context(tc.tile_pool(name="lists", bufs=1))
        sb = ctx.enter_context(tc.tile_pool(name="sb", bufs=1))
        psum = ctx.enter_context(tc.psum_pool(name="psum", bufs=1))


        scale_table = sb.tile([P, T], U8, name="scale_table", align_bytes=64)
        nc.vector.memset(scale_table[:].bitcast(I32), 0)
        word_table = sb.tile([P, T], I32, name="word_table", tag="word_table", align_bytes=64)
        words_hbm = x_words[0].rearrange("p n t -> p (n t)").bitcast(I32)
        nc.sync.dma_start(word_table[:, :T // 4], words_hbm[:, :T // 4])
        dst_list = lists.tile([P, S // 16], U16, name="dst_list")
        nc.sync.dma_start(dst_list[:], dst)
        src_list = lists.tile([P, S // 16], U16, name="src_list")
        nc.sync.dma_start(src_list[:], offs)
        for r in range(4):
            nc.sync.dma_start(scale_table[r:P:32, :].bitcast(I32), x_scales[0, r:16:4, :].bitcast(I32))
        nc.sync.dma_start(word_table[:, T // 4:], words_hbm[:, T // 4:])

        warm_in = sb.tile([P, 8], F32, name="warm_in")
        nc.vector.memset(warm_in[:], 0.0)
        warm_out = sb.tile([P, 8], F32, name="warm_out")
        nc.scalar.activation(warm_out[:], warm_in[:], ACT.Sigmoid)

        w2_raw = sb.tile([P, PACK, H], F32, name="w2_raw", tag="raw_b")
        nc.sync.dma_start(w2_raw[:], w2.rearrange("(p j) c -> p j c", j=PACK))
        w1_rows = w1.rearrange("(p j) c -> p j c", j=PACK)
        w1_raw = []
        for g in range(2):
            w1_raw.append(sb.tile([P, 2, H], F32, name="w1_raw%d" % g, tag="w1_raw%d" % g))
            nc.sync.dma_start(w1_raw[g][:], w1_rows[:, 2 * g:2 * g + 2, :])

        def gather_scales(lst, name):
            got = sb.tile([P, S], U8, name=name, align_bytes=64)
            nc.vector.tensor_copy(got[:], scale_table[:].indirect(lst[:]))
            return got

        def gather_words(lst, h, name):
            got = sb.tile([P, HALF], U32, name=name, tag=name, align_bytes=64)
            cols = HALF // 16
            nc.vector.tensor_copy(got[:], word_table[:].bitcast(U32).indirect(lst[:, h * cols:(h + 1) * cols]))
            return got

        def round_slots(rounded, raw, t0, t1, on_vector, j0=0, j1=PACK):
            src = raw[:].rearrange("p j (u t r) -> p t u j r", t=PACK, r=4)[:, t0:t1]
            to = rounded[:].rearrange("p (t u r j) -> p t u j r", t=2, r=4, j=PACK)[:, :, :, j0:j1, :]
            if on_vector:
                nc.vector.tensor_copy(to, src)
            else:
                nc.scalar.copy(to, src)

        def quantise(rounded, width, name):
            codes = sb.tile([P, width], U32, name=name + "_codes", align_bytes=64)
            scales = sb.tile([P, width], U8, name=name + "_scales", align_bytes=64)
            nc.vector.quantize_mx(out=codes[:].bitcast(FP8X4), scales=scales[:], in_=rounded[:])
            return codes, scales

        def product(bank_cols, stat, lo, words, scales):
            nc.tensor.matmul_mx(out=bank_cols, lhsT=stat[0][:, lo:lo + P].bitcast(FP8X4), lhsT_scale=stat[1][:, lo:lo + P],
                                rhs=words.bitcast(FP8X4), rhs_scale=scales, start=True, stop=True)

        dst_scales = gather_scales(dst_list, "dst_scales")
        src_scales = gather_scales(src_list, "src_scales")
        dst_words = [gather_words(dst_list, h, "dst_words%d" % h) for h in range(2)]
        src_words = [gather_words(src_list, 0, "src_words0")]

        w2_bf = [sb.tile([P, 2 * PACK * P], BF16, name="w2_bf%d" % a, align_bytes=64) for a in range(2)]
        round_slots(w2_bf[0], w2_raw, 0, 2, True)
        round_slots(w2_bf[1], w2_raw, 2, 4, False)
        w2_q = [quantise(w2_bf[a], 2 * P, "w2_q%d" % a) for a in range(2)]

        w3_raw = sb.tile([P, PACK, N], F32, name="w3_raw")
        w3_rows = w3.rearrange("(u t r) n -> r u t n", t=PACK, r=4)
        for r in range(4):
            nc.sync.dma_start(w3_raw[r:P:4, :, :], w3_rows[r])


        n_chunks = S // CHUNK
        e_bank = []
        y_bank = []

        def first_layer(bank, slot, w_q, words, scales):
            c = len(bank)
            bank.append(psum.tile([P, PACK, CHUNK], F32, name="first_layer", tag="bank%d" % slot))
            lo = (c % 2) * CHUNK
            for t in range(PACK):
                product(bank[c][:, t, :], w_q[t // 2], (t % 2) * P, words[c // 2][:, lo:lo + CHUNK], scales[:, c * CHUNK:(c + 1) * CHUNK])

        def tanh_chunk(c):
            nc.scalar.activation(e_vals[:, c], e_bank[c][:].rearrange("p t n -> p n t"), ACT.Tanh)

        for c in range(n_chunks - 1):
            first_layer(e_bank, c, w2_q, dst_words, dst_scales)

        w1_bf = [sb.tile([P, 2 * PACK * P], BF16, name="w1_bf%d" % a, tag="w1_bf%d" % a, align_bytes=64) for a in range(2)]
        for g in range(2):
            round_slots(w1_bf[0], w1_raw[g], 0, 2, True, 2 * g, 2 * g + 2)
            round_slots(w1_bf[1], w1_raw[g], 2, 4, False, 2 * g, 2 * g + 2)
        w1_q = [quantise(w1_bf[a], 2 * P, "w1_q%d" % a) for a in range(2)]
        src_words.append(gather_words(src_list, 1, "w1_bf1"))
        e_vals = sb.tile([P, n_chunks, CHUNK, PACK], F32, name="e_vals", tag="w1_raw1")
        first_layer(y_bank, 3, w1_q, src_words, src_scales)
        first_layer(y_bank, 4, w1_q, src_words, src_scales)
        tanh_chunk(0)
        first_layer(e_bank, 0, w2_q, dst_words, dst_scales)
        tanh_chunk(1)
        first_layer(y_bank, 5, w1_q, src_words, src_scales)
        w3_bf = sb.tile([P, N * PACK], BF16, name="w3_bf", tag="word_table", align_bytes=64)
        nc.gpsimd.tensor_scalar(w3_bf[:].rearrange("p (n t) -> p n t", t=PACK),
                                w3_raw[:].rearrange("p t n -> p n t"), 1.0, 0.0, ALU.mult, ALU.add)
        tanh_chunk(2)
        first_layer(y_bank, 6, w1_q, src_words, src_scales)
        tanh_chunk(3)

        z_bf = []

        def gate(c):
            z = sb.tile([P, CHUNK * PACK], BF16, name="z_bf%d" % c, align_bytes=64)
            nc.vector.scalar_tensor_tensor(z[:].rearrange("p (n t) -> p n t", t=PACK),
                                           y_bank[c][:].rearrange("p t n -> p n t"), 0.0, e_vals[:, c],
                                           ALU.max, ALU.mult)
            z_bf.append(z)

        def finish(c, w3_q):
            z_q = quantise(z_bf[c], CHUNK, "z_q%d" % c)
            o_bank = psum.tile([P, CHUNK], F32, name="o_bank", tag="bank%d" % (3 + c))
            product(o_bank[:], w3_q, 0, z_q[0][:], z_q[1][:])
            res = sb.tile([P, CHUNK], F32, name="res%d" % c)
            nc.scalar.activation(res[:], o_bank[:], ACT.Sigmoid)
            nc.sync.dma_start(out[:, c * CHUNK:(c + 1) * CHUNK], res[:])

        gate(0)
        w3_q = quantise(w3_bf, N, "w3_q")
        for c in range(1, n_chunks):
            gate(c)
            finish(c - 1, w3_q)
        finish(n_chunks - 1, w3_q)
